import numpy as np
import ml_dtypes


def mxq(x, axis, fmt="e4m3"):
    dtype, down = {"e4m3": (ml_dtypes.float8_e4m3fn, 7), "e5m2": (ml_dtypes.float8_e5m2, 14)}[fmt]
    v = np.moveaxis(np.asarray(x, np.float32).astype(ml_dtypes.bfloat16).astype(np.float64), axis, -1)
    blocks = v.reshape(v.shape[:-1] + (-1, 32))
    amax = np.abs(blocks).max(-1, keepdims=True)
    byte = np.maximum(np.where(amax > 0, np.frexp(amax)[1] - 1 + 127, 0) - down, 1)
    scale = np.exp2(byte - 127.0)
    codes = (blocks / scale).astype(np.float32).astype(dtype).astype(np.float64)
    return np.moveaxis((codes * scale).reshape(v.shape), -1, axis)


WIDE = False


def mx_kscale(k):
    if not WIDE:
        return np.ones(k)
    levels = np.array([10, -10, 5, -5, 0])
    if k % 512:
        return np.exp2(np.random.permutation(np.resize(levels, k // 32))).repeat(32)
    a = np.empty((k // 512, 16))
    for p in range(k // 512):
        a[p, :8] = np.random.permutation(np.resize(levels, 8))
        for g in range(8):
            far = levels[np.abs(levels - a[p, g]) >= 10]
            a[p, g + 8] = far[np.random.randint(len(far))]
    return np.exp2(a.ravel()).repeat(32)


def f64(x):
    return np.asarray(x).astype(np.float64)


def striped(idx):
    return np.tile(idx.reshape(-1, 16).T, (8, 1)).astype(np.uint16)


def unstriped(offs):
    return offs[:16].T.reshape(-1).astype(np.int64)


def pack_weight(w):
    k, n = w.shape
    w = f64(np.asarray(w, np.float32).astype(ml_dtypes.bfloat16)).reshape(k // 32, 32, n)
    amax = np.abs(w).max(1)
    byte = np.clip(np.where(amax > 0, np.frexp(amax)[1] - 1 + 127 - 7, 1), 1, 254)
    scaled = (w * np.exp2(127.0 - byte)[:, None, :]).reshape(k, n).astype(np.float32)
    words = np.ascontiguousarray(scaled.reshape(k // 512, 128, 4, n).transpose(0, 1, 3, 2)).astype(ml_dtypes.float8_e4m3fn).view(np.uint8)
    return words, np.ascontiguousarray(byte.astype(np.uint8).reshape(k // 512, 16, n))


def unpack_weight(words, scales):
    g, p, n, _ = words.shape
    vals = np.ascontiguousarray(words).view(ml_dtypes.float8_e4m3fn).astype(np.float64) * np.repeat(np.exp2(scales.astype(np.float64) - 127.0), 8, axis=1)[..., None]
    return vals.transpose(0, 1, 3, 2).reshape(g * 512, n)


K, T, S, D, N = 512, 2048, 1024, 8, 256
P = 2 ** 7


def setup_inputs():
    n = np.random.standard_normal
    s = mx_kscale(K)[:, None]
    packed_xT = pack_weight(n((K, T)) * s)
    return {
        "x_words": packed_xT[0],
        "x_scales": packed_xT[1],
        "w1": (n((K, N)) / np.sqrt(K) / s).astype(np.float32),
        "w2": (n((K, N)) / np.sqrt(K) / s).astype(np.float32),
        "w3": (n((K, N)) / np.sqrt(K) / s).astype(np.float32),
        "win": (np.tile(np.random.uniform(0.3, 1.0, S), (P, 1))).astype(np.float32),
        "offs": striped(np.random.permutation(T)[:S]),
    }


def reference(x_words, x_scales, w1, w2, w3, win, offs):
    xq = unpack_weight(x_words, x_scales)[:, unstriped(offs)]
    gx = mxq(f64(w1), 0, "e4m3").T @ xq
    gy = mxq(f64(w2), 0, "e4m3").T @ xq
    sxyj = (f64(win)[:1] * gx) * gy
    sxy = sxyj.reshape(len(sxyj), -1, D).sum(axis=2)
    gt = mxq(f64(w3), 0, "e4m3").T @ xq
    sytj = (f64(win)[:1] * gy) * gt
    syt = sytj.reshape(len(sytj), -1, D).sum(axis=2)
    syyj = f64(win)[:1] * ((gy) ** 2)
    syy = syyj.reshape(len(syyj), -1, D).sum(axis=2)
    sxtj = (f64(win)[:1] * gx) * gt
    sxt = sxtj.reshape(len(sxtj), -1, D).sum(axis=2)
    sxxj = f64(win)[:1] * ((gx) ** 2)
    sxx = sxxj.reshape(len(sxxj), -1, D).sum(axis=2)
    det = (sxx + 0.2) * (syy + 0.2) - ((sxy) ** 2)
    return (sxy * syt - ((syy + 0.2) * sxt)) / (det + 0.1)

from contextlib import ExitStack

import concourse.mybir as mybir
from concourse.masks import make_identity

K, T, S, D, N = 512, 2048, 1024, 8, 256
V = S // D
P = 128
PACK = 4
FLOPS = 3 * 2 * K * N * S

F32 = mybir.dt.float32
BF16 = mybir.dt.bfloat16
I32 = mybir.dt.int32
U32 = mybir.dt.uint32
U16 = mybir.dt.uint16
U8 = mybir.dt.uint8
FP8X4 = mybir.dt.float8_e4m3fn_x4
ALU = mybir.AluOpType
ACT = mybir.ActivationFunctionType
RIDGE = 0.2
DET_SHIFT = 0.1
HALVES = N // P
DIRECT = 2


def tile_picked_ylukan_flow_p_kernel(tc, x_words, x_scales, w1, w2, w3, win, offs, out):
    nc = tc.nc
    with ExitStack() as ctx:
        keep = ctx.enter_context(tc.tile_pool(name="keep", bufs=1))
        ring = ctx.enter_context(tc.tile_pool(name="ring", bufs=3))
        grads = ctx.enter_context(tc.psum_pool(name="grads", bufs=2))
        sums = ctx.enter_context(tc.psum_pool(name="sums", bufs=1))

        offsets = keep.tile([P, S // 16], U16, name="offsets")
        nc.sync.dma_start(offsets[:], offs)

        scale_table = keep.tile([P, T], U8, name="scale_table", align_bytes=64)
        nc.vector.memset(scale_table[:].bitcast(I32), 0)
        for q in range(4):
            nc.sync.dma_start(scale_table[32 * q : 32 * q + 4, :].bitcast(I32), x_scales[0, 4 * q : 4 * q + 4, :].bitcast(I32))

        raw = [keep.tile([P, PACK, N], F32, name="raw%d" % i) for i in range(3)]
        word_table = keep.tile([P, T], U32, name="word_table", align_bytes=64)
        weight = keep.tile([P, D], F32, name="weight")
        nc.sync.dma_start(raw[0][:], w1.rearrange("(p t) m -> p t m", t=PACK))
        nc.sync.dma_start(word_table[:].bitcast(I32), x_words[0].rearrange("p c t -> p (c t)").bitcast(I32))
        nc.sync.dma_start(raw[1][:], w2.rearrange("(p t) m -> p t m", t=PACK))
        nc.sync.dma_start(raw[2][:], w3.rearrange("(p t) m -> p t m", t=PACK))
        nc.sync.dma_start(weight[:], win[0:1, :].rearrange("o (v d) -> (o v) d", d=D))

        identity = keep.tile([P, P], F32, name="identity")
        make_identity(nc, identity[:])

        picked_scales = keep.tile([P, S], U8, name="picked_scales", align_bytes=64)
        nc.vector.tensor_copy(picked_scales[:], scale_table[:].indirect(offsets[:]))
        x_scale = keep.tile([P, S], U8, name="x_scale", align_bytes=64)
        nc.vector.tensor_copy(
            x_scale[:].rearrange("p (h e v) -> p h v e", h=2, e=4),
            picked_scales[:].rearrange("p (v h e) -> p h v e", h=2, e=4),
        )

        grouped = [keep.tile([P, N * PACK], BF16, name="grouped%d" % i, align_bytes=64) for i in range(3)]

        def interleave(copy, i, lo, hi):
            copy(
                grouped[i][:, lo * PACK : hi * PACK].rearrange("p (c j t) -> p c t j", j=4, t=PACK),
                raw[i][:, :, lo:hi].rearrange("p t (c j) -> p c t j", j=4),
            )

        wxy_code = keep.tile([P, 2 * N], U32, name="wxy_code", align_bytes=64)
        wxy_scale = keep.tile([P, 2 * N], U8, name="wxy_scale", align_bytes=64)
        wt_code = keep.tile([P, N], U32, name="wt_code", align_bytes=64)
        wt_scale = keep.tile([P, N], U8, name="wt_scale", align_bytes=64)

        interleave(nc.scalar.copy, 0, 0, N)
        nc.vector.quantize_mx(wxy_code[:, 0:N].bitcast(FP8X4), wxy_scale[:, 0:N], grouped[0][:])

        picked_words = keep.tile([P, S], U32, name="picked_words", align_bytes=64)
        nc.vector.tensor_copy(picked_words[:], word_table[:].indirect(offsets[:]))
        x_code = [keep.tile([P, S // 2], U32, name="x_code%d" % h, align_bytes=64) for h in range(2)]

        def deal_words(h):
            nc.vector.tensor_copy(
                x_code[h][:].rearrange("p (e v) -> p v e", e=4),
                picked_words[:].rearrange("p (v h e) -> p h v e", h=2, e=4)[:, h],
            )

        deal_words(0)
        interleave(nc.scalar.copy, 1, 0, N)
        nc.vector.quantize_mx(wxy_code[:, N : 2 * N].bitcast(FP8X4), wxy_scale[:, N : 2 * N], grouped[1][:])
        interleave(nc.scalar.copy, 2, 0, N // 2)
        interleave(nc.vector.tensor_copy, 2, N // 2, N)
        deal_words(1)
        nc.vector.quantize_mx(wt_code[:].bitcast(FP8X4), wt_scale[:], grouped[2][:])

        def products(pair):
            gxy = [grads.tile([P, 2 * N], F32, name="gxy", tag="gxy", bufs=4) for u in range(2)]
            gt = grads.tile([P, 2 * N], F32, name="gt", tag="gt", bufs=2)
            for u in range(2):
                d = 2 * pair + u
                code = x_code[d // 4][:, (d % 4) * V : (d % 4 + 1) * V].bitcast(FP8X4)
                scale = x_scale[:, d * V : (d + 1) * V]
                nc.tensor.matmul_mx(gxy[u][:], lhsT=code, lhsT_scale=scale, rhs=wxy_code[:].bitcast(FP8X4), rhs_scale=wxy_scale[:], start=True, stop=True)
            for u in range(2):
                d = 2 * pair + u
                code = x_code[d // 4][:, (d % 4) * V : (d % 4 + 1) * V].bitcast(FP8X4)
                scale = x_scale[:, d * V : (d + 1) * V]
                nc.tensor.matmul_mx(gt[:, u * N : (u + 1) * N], lhsT=code, lhsT_scale=scale, rhs=wt_code[:].bitcast(FP8X4), rhs_scale=wt_scale[:], start=True, stop=True)
            return gxy, gt

        sum_x = sums.tile([P, 2 * N], F32, name="sum_x")
        sum_t = sums.tile([P, 2 * N], F32, name="sum_t")
        yy_run = keep.tile([P, N], F32, name="yy_run")
        yy_last = [keep.tile([P, N], F32, name="yy_last%d" % i) for i in range(DIRECT)]

        def add_turned(bank, terms, first, last):
            blocks = terms.shape[1] // P
            for b in range(blocks):
                nc.tensor.matmul(
                    bank[:, b * P : (b + 1) * P], terms[:, b * P : (b + 1) * P], identity[:],
                    is_transpose=True, start=(first and b == 0), stop=(last and b == blocks - 1),
                )

        def square_term(d, gxy):
            square = ring.tile([P, N], F32, name="square")
            nc.scalar.activation(square[:], gxy[:, N : 2 * N], ACT.Square)
            w = weight[:, d : d + 1]
            if d == 0:
                nc.gpsimd.tensor_scalar(yy_run[:], square[:], w, RIDGE, ALU.mult, ALU.add)
            elif d >= D - DIRECT:
                nc.gpsimd.tensor_scalar(yy_last[d - (D - DIRECT)][:], square[:], w, 0.0, ALU.mult, ALU.add)
            else:
                term = ring.tile([P, N], F32, name="term")
                nc.gpsimd.tensor_scalar(term[:], square[:], w, 0.0, ALU.mult, ALU.add)
                nc.gpsimd.tensor_tensor(yy_run[:], yy_run[:], term[:], ALU.add)

        def window_terms(d, g):
            u = d % 2
            gxy = g[0][u][:]
            gt = g[1][:, u * N : (u + 1) * N]
            weighted = ring.tile([P, 2 * N], F32, name="weighted")
            nc.scalar.activation(weighted[:], gxy, ACT.Copy, scale=weight[:, d : d + 1])
            if d > 0:
                square_term(d, gxy)
            x_terms = ring.tile([P, 2 * N], F32, name="x_terms")
            nc.vector.tensor_tensor(
                x_terms[:].rearrange("p (a m) -> p a m", a=2),
                weighted[:, 0:N].unsqueeze(1).broadcast_to([P, 2, N]),
                gxy.rearrange("p (a m) -> p a m", a=2), ALU.mult,
            )
            if d == 0:
                square_term(d, gxy)
            t_terms = ring.tile([P, 2 * N], F32, name="t_terms")
            nc.vector.tensor_tensor(
                t_terms[:].rearrange("p (a m) -> p a m", a=2),
                weighted[:].rearrange("p (a m) -> p a m", a=2),
                gt.unsqueeze(1).broadcast_to([P, 2, N]), ALU.mult,
            )
            if d == D - 1:
                sum_y = grads.tile([P, 2 * N], F32, name="sum_y", tag="gt", bufs=2)
                add_turned(sum_y[:, 0:N], yy_run[:], True, False)
                for i in range(DIRECT):
                    add_turned(sum_y[:, 0:N], yy_last[i][:], False, i == DIRECT - 1)
                closed.append(sum_y)
            add_turned(sum_x, x_terms[:], d == 0, d == D - 1)
            add_turned(sum_t, t_terms[:], d == 0, d == D - 1)

        closed = []
        pairs = D // 2
        g_of = {0: products(0), 1: products(1)}
        for pair in range(pairs):
            for u in range(2):
                window_terms(2 * pair + u, g_of[pair])
            if pair + 2 < pairs:
                g_of[pair + 2] = products(pair + 2)

        sum_y = closed[0]
        factors = keep.tile([P, 2, N], F32, name="factors")
        xy_square = keep.tile([P, N], F32, name="xy_square")
        halves = range(HALVES)
        cols = [slice(h * P, (h + 1) * P) for h in halves]

        def half_tiles(name, width):
            return [keep.tile([P, width], F32, name="%s%d" % (name, h)) for h in halves]

        diag = half_tiles("diag", P)
        cross = half_tiles("cross", 2 * P)
        ratio = half_tiles("ratio", 2 * P)
        root = half_tiles("root", P)
        guess_abs = half_tiles("guess_abs", P)
        sign = half_tiles("sign", P)
        result = half_tiles("result", P)
        t_sums = sum_t[:].rearrange("p (a m) -> p a m", a=2)

        nc.scalar.copy(factors[:, 0, :], sum_y[:, 0:N])
        nc.scalar.activation(xy_square[:], sum_x[:, N : 2 * N], ACT.Square)
        nc.scalar.copy(factors[:, 1, :], sum_x[:, N : 2 * N])
        for h in halves:
            nc.vector.scalar_tensor_tensor(diag[h][:], sum_x[:, cols[h]], RIDGE, factors[:, 0, cols[h]], ALU.add, ALU.mult)
        for h in halves:
            nc.vector.scalar_tensor_tensor(ratio[h][:, P : 2 * P], diag[h][:], DET_SHIFT, xy_square[:, cols[h]], ALU.add, ALU.subtract)
        for h in halves:
            nc.scalar.activation(root[h][:], ratio[h][:, P : 2 * P], ACT.Abs_reciprocal_sqrt)
            nc.scalar.activation(sign[h][:], ratio[h][:, P : 2 * P], ACT.Sign)
            nc.scalar.activation(guess_abs[h][:], root[h][:], ACT.Square)
        for h in halves:
            nc.vector.tensor_tensor(cross[h][:].rearrange("p (a m) -> p a m", a=2), factors[:, :, cols[h]], t_sums[:, :, cols[h]], ALU.mult)
        signed = half_tiles("signed", P)
        for h in halves:
            nc.vector.tensor_tensor(ratio[h][:, 0:P], cross[h][:, P : 2 * P], cross[h][:, 0:P], ALU.subtract)
        for h in halves:
            nc.vector.tensor_tensor(signed[h][:], ratio[h][:, 0:P], sign[h][:], ALU.mult)
        for h in halves:
            nc.vector.tensor_tensor(result[h][:], signed[h][:], guess_abs[h][:], ALU.mult)
            nc.sync.dma_start(out[cols[h], :], result[h][:])
